import numpy as np
import ml_dtypes


def mxq(x, axis, fmt="e4m3"):
    dtype, down = {"e4m3": (ml_dtypes.float8_e4m3fn, 7), "e5m2": (ml_dtypes.float8_e5m2, 14)}[fmt]
    v = np.moveaxis(np.asarray(x, np.float32).astype(ml_dtypes.bfloat16).astype(np.float64), axis, -1)
    blocks = v.reshape(v.shape[:-1] + (-1, 32))
    amax = np.abs(blocks).max(-1, keepdims=True)
    byte = np.maximum(np.where(amax > 0, np.frexp(amax)[1] - 1 + 127, 0) - down, 1)
    scale = np.exp2(byte - 127.0)
    codes = (blocks / scale).astype(np.float32).astype(dtype).astype(np.float64)
    return np.moveaxis((codes * scale).reshape(v.shape), -1, axis)


WIDE = False


def mx_kscale(k):
    if not WIDE:
        return np.ones(k)
    levels = np.array([10, -10, 5, -5, 0])
    if k % 512:
        return np.exp2(np.random.permutation(np.resize(levels, k // 32))).repeat(32)
    a = np.empty((k // 512, 16))
    for p in range(k // 512):
        a[p, :8] = np.random.permutation(np.resize(levels, 8))
        for g in range(8):
            far = levels[np.abs(levels - a[p, g]) >= 10]
            a[p, g + 8] = far[np.random.randint(len(far))]
    return np.exp2(a.ravel()).repeat(32)


BF16 = ml_dtypes.bfloat16


def bf(x):
    return np.asarray(x, np.float32).astype(BF16)


def f64(x):
    return np.asarray(x).astype(np.float64)

E4M3FN = np.array([(-1.0 if i & 128 else 1.0) * ((1.0 + (i & 7) / 8.0) * 2.0 ** (((i >> 3) & 15) - 7) if i & 120 else (i & 7) * 2.0 ** -9) for i in range(256)])


def e4m3fn_bytes(y):
    return np.clip(np.asarray(y, np.float64), -448.0, 448.0).astype(np.float32).astype(ml_dtypes.float8_e4m3fn).view(np.uint8)


def e4m3fn_values(b):
    return E4M3FN[b]


U, I = 1024, 2048


def setup_inputs():
    s = mx_kscale(I)
    touched = np.random.random_sample((U, I)) < 0.5
    strength = touched * (0.5 + np.random.random_sample((U, I)))
    seen = touched & (np.random.random_sample((U, I)) < 0.5)
    gain = np.exp(0.4 * np.random.standard_normal((I, 1)))
    B = 0.8 * np.random.standard_normal((I, I)) * gain / np.sqrt(I) / s[:, None]
    B_scale = (np.abs(B).max(axis=1, keepdims=True) / 448).astype(np.float32)
    return {"r": bf(strength * s),
            "B_bytes": e4m3fn_bytes(B / f64(B_scale)),
            "B_scale": B_scale,
            "bias": bf(0.3 * np.random.standard_normal(I)),
            "seen": bf(seen)}


def reference(r, B_bytes, B_scale, bias, seen):
    B = e4m3fn_values(B_bytes) * np.repeat(f64(B_scale), I, axis=1)
    z = mxq(f64(r), 1, "e4m3") @ mxq(B, 0, "e4m3")
    p = np.exp(z + f64(bias)) * (1 - f64(seen))
    return p

@@ -1,0 +1,254 @@
+from contextlib import ExitStack
+
+import concourse.mybir as mybir
+from concourse.masks import make_identity
+
+U, I = 1024, 2048
+FLOPS = 2 * U * I * I
+
+F32 = mybir.dt.float32
+BF16 = mybir.dt.bfloat16
+U32 = mybir.dt.uint32
+I32 = mybir.dt.int32
+U8 = mybir.dt.uint8
+FP8 = mybir.dt.float8_e4m3fn
+FP8X4 = mybir.dt.float8_e4m3fn_x4
+MULT = mybir.AluOpType.mult
+ADD = mybir.AluOpType.add
+SUB = mybir.AluOpType.subtract
+ACT = mybir.ActivationFunctionType
+
+P = 128
+PACK = 4
+GROUPS = I // (P * PACK)
+USERS = U // P
+CHUNKS = [(0, 256), (256, 512), (768, 512), (1280, 512), (1792, 256)]
+SEEN_CUTS = [(0, 768), (768, 1280)]
+MASK = 4096.0
+V_PLANES = [(0, 1), (), (), (), ()]
+
+
+def tile_masked_item_recommender_d3_kernel(tc, r, B_bytes, B_scale, bias, seen, out):
+    nc = tc.nc
+    with ExitStack() as ctx:
+        const = ctx.enter_context(tc.tile_pool(name="const", bufs=1))
+        keep = ctx.enter_context(tc.tile_pool(name="keep", bufs=1))
+        raws = ctx.enter_context(tc.tile_pool(name="raws", bufs=6))
+        stage = ctx.enter_context(tc.tile_pool(name="stage", bufs=3))
+        outs = ctx.enter_context(tc.tile_pool(name="outs", bufs=6))
+        psum = ctx.enter_context(tc.psum_pool(name="psum", bufs=8))
+
+        ident = const.tile([P, P], F32, name="ident")
+        make_identity(nc, ident[:])
+        ones = const.tile([P, P], BF16, name="ones")
+        nc.vector.memset(ones[:], 1.0)
+        bias_row = const.tile([P, I], BF16, name="bias_row")
+        nc.vector.memset(bias_row[:].bitcast(I32), 0)
+
+        sc = const.tile([P, GROUPS * PACK], F32, name="sc")
+        bytes_view = B_bytes.rearrange("(g p t) n -> g p t n", p=P, t=PACK)
+        b_raw = {}
+
+        def load_bytes(c, g):
+            n0, w = CHUNKS[c]
+            t8 = keep.tile([P, PACK, w], U8, name="b_raw%d_%d" % (c, g), align_bytes=64)
+            nc.sync.dma_start(out=t8[:], in_=bytes_view[g][:, :, n0:n0 + w])
+            b_raw[c, g] = t8
+
+        r_raw = {}
+
+        def load_r(u):
+            t = raws.tile([P, I], BF16, name="r_raw")
+            nc.sync.dma_start(out=t[:], in_=r[u * P:(u + 1) * P, :])
+            r_raw[u] = t
+
+        w_t = {}
+
+        def load_seen(s, u):
+            n0, w = SEEN_CUTS[s]
+            t = keep.tile([P, w], BF16, name="seen%d_%d" % (s, u))
+            nc.sync.dma_start(out=t[:], in_=seen[u * P:(u + 1) * P, n0:n0 + w])
+            w_t[s, u] = t
+
+        nc.sync.dma_start(out=sc[:].rearrange("p (g t) -> p g t", t=PACK),
+                          in_=B_scale.rearrange("(g p t) o -> p g (t o)", p=P, t=PACK))
+        for g in range(GROUPS):
+            load_bytes(0, g)
+        nc.sync.dma_start(out=bias_row[0:1, :], in_=bias.rearrange("(o n) -> o n", o=1))
+        load_r(0)
+        load_r(1)
+        load_seen(0, 0)
+        load_bytes(1, 0)
+        load_r(2)
+        load_seen(0, 1)
+        load_bytes(1, 1)
+        load_r(3)
+        load_seen(0, 2)
+        load_r(4)
+        load_bytes(1, 2)
+        load_seen(0, 3)
+        load_r(5)
+        load_bytes(1, 3)
+        load_seen(0, 4)
+        load_seen(0, 5)
+
+        late = [lambda: load_r(6), lambda: load_seen(0, 6), lambda: load_r(7), lambda: load_seen(0, 7)]
+        late += [lambda g=g: load_bytes(2, g) for g in range(GROUPS)]
+        for u in range(USERS):
+            late.append(lambda u=u: load_seen(1, u))
+            if u % 2 == 1:
+                late.append(lambda g=u // 2: load_bytes(3, g))
+        late += [lambda g=g: load_bytes(4, g) for g in range(GROUPS)]
+
+        b_codes, b_scales, wide_t, grp_t = {}, {}, {}, {}
+        for c, (n0, w) in enumerate(CHUNKS):
+            bct = keep.tile([P, GROUPS, w], U32, name="b_codes%d" % c, align_bytes=64)
+            bst = keep.tile([P, GROUPS, w], U8, name="b_scales%d" % c, align_bytes=64)
+            b_codes[c], b_scales[c] = bct, bst
+
+        def widen(c, g, planes):
+            n0, w = CHUNKS[c]
+            if (c, g) not in wide_t:
+                t = stage.tile([P, PACK, w], BF16, name="wide", align_bytes=64)
+                wide_t[c, g] = t
+            for t in planes:
+                j = g * PACK + t
+                src = b_raw[c, g][:, t, :].bitcast(FP8)
+                dst = wide_t[c, g][:, t, :]
+                if t in V_PLANES[c]:
+                    nc.vector.tensor_scalar(out=dst, in0=src, scalar1=sc[:, j:j + 1], scalar2=None, op0=MULT)
+                else:
+                    nc.scalar.activation(out=dst, in_=src, func=ACT.Copy, scale=sc[:, j:j + 1])
+
+        def interleave(c, g):
+            n0, w = CHUNKS[c]
+            t = stage.tile([P, w, PACK], BF16, name="grp", align_bytes=64)
+            nc.vector.tensor_copy(out=t[:].rearrange("p (c i) t -> p c t i", i=4),
+                                  in_=wide_t[c, g][:].rearrange("p t (c i) -> p c t i", i=4))
+            grp_t[c, g] = t
+
+        def quant(c, g):
+            nc.vector.quantize_mx(out=b_codes[c][:, g, :].bitcast(FP8X4), scales=b_scales[c][:, g, :],
+                                  in_=grp_t[c, g][:].rearrange("p n t -> p (n t)"))
+
+        r_codes, r_scales, tp_t, rg_t = {}, {}, {}, {}
+
+        def transposes(u):
+            words = r_raw[u][:].bitcast(F32)
+            for h in range(2):
+                tp = psum.tile([P, 2, 2, P], F32, name="ps")
+                for gg in range(2):
+                    for e in range(2):
+                        k0 = 256 * (2 * h + gg)
+                        nc.tensor.transpose(tp[:, gg, e, :], words[:, k0 + e:k0 + 256:2], ident[:])
+                tp_t[u, h] = tp
+
+        def copy_r(u, h):
+            if h == 0:
+                t = stage.tile([P, 2, 2 * P * PACK], BF16, name="r_grp", align_bytes=64)
+                rg_t[u] = t
+            dst = rg_t[u][:, h, :].bitcast(F32).rearrange("p (g n e) -> p g n e", g=2, e=2)
+            nc.scalar.copy(out=dst, in_=tp_t[u, h][:].rearrange("p g e n -> p g n e"))
+
+        def quant_r(u):
+            ct = keep.tile([P, GROUPS, P], U32, name="r_codes%d" % u, align_bytes=64)
+            st = keep.tile([P, GROUPS, P], U8, name="r_scales%d" % u, align_bytes=64)
+            nc.vector.quantize_mx(out=ct[:].rearrange("p g n -> p (g n)").bitcast(FP8X4),
+                                  scales=st[:].rearrange("p g n -> p (g n)"),
+                                  in_=rg_t[u][:].rearrange("p h x -> p (h x)"))
+            r_codes[u], r_scales[u] = ct, st
+
+        ub = const.tile([P, I], BF16, name="ub")
+
+        def spread_bias():
+            for q in range(4):
+                ps = psum.tile([P, 512], F32, name="ps")
+                nc.tensor.matmul(ps[:], lhsT=ones[:], rhs=bias_row[:, 512 * q:512 * q + 512], start=True, stop=True)
+                nc.vector.tensor_scalar(out=ub[:, 512 * q:512 * q + 512], in0=ps[:], scalar1=1.0 / MASK, scalar2=None, op0=MULT)
+
+        def mask(s, u):
+            n0, w = SEEN_CUTS[s]
+            nc.vector.tensor_tensor(out=w_t[s, u][:], in0=ub[:, n0:n0 + w], in1=w_t[s, u][:], op=SUB)
+
+        z_t, a_t = {}, {}
+
+        def mm(c, u):
+            n0, w = CHUNKS[c]
+            z = psum.tile([P, 512], F32, name="ps")
+            for g in range(GROUPS):
+                nc.tensor.matmul_mx(out=z[:, 0:w],
+                                    lhsT=r_codes[u][:, g, :].bitcast(FP8X4), lhsT_scale=r_scales[u][:, g, :],
+                                    rhs=b_codes[c][:, g, :].bitcast(FP8X4), rhs_scale=b_scales[c][:, g, :],
+                                    start=(g == 0), stop=(g == GROUPS - 1))
+            z_t[c, u] = z
+
+        def add(c, u):
+            n0, w = CHUNKS[c]
+            s = 0 if n0 < 768 else 1
+            off = n0 - SEEN_CUTS[s][0]
+            a = outs.tile([P, 512], F32, name="arg")
+            nc.vector.scalar_tensor_tensor(out=a[:, 0:w], in0=z_t[c, u][:, 0:w], scalar=1.0 / MASK,
+                                           in1=w_t[s, u][:, off:off + w], op0=MULT, op1=ADD)
+            a_t[c, u] = a
+
+        def expo(c, u):
+            n0, w = CHUNKS[c]
+            o = outs.tile([P, 512], F32, name="res")
+            nc.scalar.activation(out=o[:, 0:w], in_=a_t[c, u][:, 0:w], func=ACT.Exp, scale=MASK)
+            nc.sync.dma_start(out=out[u * P:(u + 1) * P, n0:n0 + w], in_=o[:, 0:w])
+
+        for g in range(GROUPS):
+            widen(0, g, range(4))
+            if g >= 1:
+                interleave(0, g - 1)
+            if g >= 2:
+                quant(0, g - 2)
+        transposes(0)
+        copy_r(0, 0)
+        copy_r(0, 1)
+        interleave(0, 3)
+        quant(0, 2)
+        spread_bias()
+        quant(0, 3)
+        quant_r(0)
+        mask(0, 0)
+
+        prev = None
+        for c in range(len(CHUNKS)):
+            for u in range(USERS):
+                if late:
+                    late.pop(0)()
+                    if c == 0 and late:
+                        late.pop(0)()
+                nxt = c + 1 if c + 1 < len(CHUNKS) else None
+                g, half = u // 2, u % 2
+                if c == 0 and u + 1 < USERS:
+                    transposes(u + 1)
+                    copy_r(u + 1, 0)
+                    copy_r(u + 1, 1)
+                mm(c, u)
+                if nxt is not None:
+                    widen(nxt, g, (0, 1) if half == 0 else (2, 3))
+                if prev is not None:
+                    add(*prev)
+                if c == 0 and u + 1 < USERS:
+                    mask(0, u + 1)
+                    quant_r(u + 1)
+                if c == 1:
+                    mask(1, u)
+                if nxt is not None:
+                    if half == 0 and g >= 1:
+                        interleave(nxt, g - 1)
+                    if half == 1 and g >= 1:
+                        quant(nxt, g - 1)
+                if prev is not None:
+                    expo(*prev)
+                prev = (c, u)
+            if nxt is not None:
+                interleave(nxt, GROUPS - 1)
+                add(*prev)
+                quant(nxt, GROUPS - 1)
+                expo(*prev)
+                prev = None
+        add(*prev)
+        expo(*prev)

@@ -16,16 +16,29 @@ FP8X4 = mybir.dt.float8_e4m3fn_x4
 MULT = mybir.AluOpType.mult
 ADD = mybir.AluOpType.add
 SUB = mybir.AluOpType.subtract
+IS_EQUAL = mybir.AluOpType.is_equal
 ACT = mybir.ActivationFunctionType
 
 P = 128
 PACK = 4
 GROUPS = I // (P * PACK)
 USERS = U // P
+HALF = 4
 CHUNKS = [(0, 256), (256, 512), (768, 512), (1280, 512), (1792, 256)]
-SEEN_CUTS = [(0, 768), (768, 1280)]
+TURNED = (1, 2)
+D_CUTS = {0: (0, 256), 3: (1280, 768), 4: (1280, 768)}
+T0, TW = 256, 1024
 MASK = 4096.0
-V_PLANES = [(0, 1), (), (), (), ()]
+LEAD = 2
+LAG_ADD = 1
+LAG_EXP = 3
+LAG_TE = 1
+LAG_TT = 3
+LAG_TM = 3
+TLEAD = 2
+PAIR = 2
+B_BUFS = 13
+V_PLANES = [(0, 1), (), (0,), (), ()]
 
 
 def tile_masked_item_recommender_d3_kernel(tc, r, B_bytes, B_scale, bias, seen, out):
@@ -34,14 +47,18 @@ def tile_masked_item_recommender_d3_kernel(tc, r, B_bytes, B_scale, bias, seen, 
         const = ctx.enter_context(tc.tile_pool(name="const", bufs=1))
         keep = ctx.enter_context(tc.tile_pool(name="keep", bufs=1))
         raws = ctx.enter_context(tc.tile_pool(name="raws", bufs=6))
+        braws = ctx.enter_context(tc.tile_pool(name="braws", bufs=B_BUFS))
         stage = ctx.enter_context(tc.tile_pool(name="stage", bufs=3))
         outs = ctx.enter_context(tc.tile_pool(name="outs", bufs=6))
+        outs2 = ctx.enter_context(tc.tile_pool(name="outs2", bufs=2))
         psum = ctx.enter_context(tc.psum_pool(name="psum", bufs=8))
 
         ident = const.tile([P, P], F32, name="ident")
         make_identity(nc, ident[:])
-        ones = const.tile([P, P], BF16, name="ones")
-        nc.vector.memset(ones[:], 1.0)
+        small = const.tile([P, P], BF16, name="small")
+        nc.gpsimd.memset(small[:], 1.0 / MASK)
+        one = const.tile([P, 2], BF16, name="one")
+        nc.gpsimd.memset(one[:], 1.0)
         bias_row = const.tile([P, I], BF16, name="bias_row")
         nc.vector.memset(bias_row[:].bitcast(I32), 0)
 
@@ -51,8 +68,8 @@ def tile_masked_item_recommender_d3_kernel(tc, r, B_bytes, B_scale, bias, seen, 
 
         def load_bytes(c, g):
             n0, w = CHUNKS[c]
-            t8 = keep.tile([P, PACK, w], U8, name="b_raw%d_%d" % (c, g), align_bytes=64)
-            nc.sync.dma_start(out=t8[:], in_=bytes_view[g][:, :, n0:n0 + w])
+            t8 = braws.tile([P, PACK, 512], U8, name="b_raw", align_bytes=64)
+            nc.sync.dma_start(out=t8[:, :, 0:w], in_=bytes_view[g][:, :, n0:n0 + w])
             b_raw[c, g] = t8
 
         r_raw = {}
@@ -64,40 +81,50 @@ def tile_masked_item_recommender_d3_kernel(tc, r, B_bytes, B_scale, bias, seen, 
 
         w_t = {}
 
-        def load_seen(s, u):
-            n0, w = SEEN_CUTS[s]
-            t = keep.tile([P, w], BF16, name="seen%d_%d" % (s, u))
+        def load_seen(c, u):
+            n0, w = D_CUTS[c]
+            t = keep.tile([P, w], BF16, name="seen%d_%d" % (c, u))
             nc.sync.dma_start(out=t[:], in_=seen[u * P:(u + 1) * P, n0:n0 + w])
-            w_t[s, u] = t
+            w_t[c, u] = t
 
-        nc.sync.dma_start(out=sc[:].rearrange("p (g t) -> p g t", t=PACK),
-                          in_=B_scale.rearrange("(g p t) o -> p g (t o)", p=P, t=PACK))
+        seen_t = []
+        for h in range(2):
+            sth = keep.tile([P, HALF, TW], BF16, name="seen_t%d" % h)
+            seen_t.append(sth)
+
+        def load_seen_t(h, q):
+            u = HALF * h + q
+            nc.sync.dma_start(out=seen_t[h][:, q, :], in_=seen[u * P:(u + 1) * P, T0:T0 + TW])
+
+        nc.scalar.dma_start(out=sc[:].rearrange("p (g t) -> p g t", t=PACK),
+                            in_=B_scale.rearrange("(g p t) o -> p g (t o)", p=P, t=PACK))
         for g in range(GROUPS):
             load_bytes(0, g)
         nc.sync.dma_start(out=bias_row[0:1, :], in_=bias.rearrange("(o n) -> o n", o=1))
         load_r(0)
+        load_bytes(1, 0)
         load_r(1)
         load_seen(0, 0)
-        load_bytes(1, 0)
         load_r(2)
-        load_seen(0, 1)
         load_bytes(1, 1)
+        load_seen(0, 1)
         load_r(3)
+        load_bytes(1, 2)
         load_seen(0, 2)
         load_r(4)
-        load_bytes(1, 2)
-        load_seen(0, 3)
-        load_r(5)
         load_bytes(1, 3)
-        load_seen(0, 4)
-        load_seen(0, 5)
+        load_seen(0, 3)
 
-        late = [lambda: load_r(6), lambda: load_seen(0, 6), lambda: load_r(7), lambda: load_seen(0, 7)]
-        late += [lambda g=g: load_bytes(2, g) for g in range(GROUPS)]
+        late = [lambda: load_r(5), lambda: load_seen(0, 4), lambda: load_r(6), lambda: load_seen(0, 5), lambda: load_r(7),
+                lambda: load_seen(0, 6), lambda: load_seen(0, 7)]
+        for g in range(GROUPS):
+            late.append(lambda g=g: load_bytes(2, g))
+            late.append(lambda q=g: load_seen_t(0, q))
+        late += [lambda q=q: load_seen_t(1, q) for q in range(HALF)]
         for u in range(USERS):
-            late.append(lambda u=u: load_seen(1, u))
-            if u % 2 == 1:
+            if u % 2 == 0:
                 late.append(lambda g=u // 2: load_bytes(3, g))
+            late.append(lambda u=u: load_seen(3, u))
         late += [lambda g=g: load_bytes(4, g) for g in range(GROUPS)]
 
         b_codes, b_scales, wide_t, grp_t = {}, {}, {}, {}
@@ -113,7 +140,7 @@ def tile_masked_item_recommender_d3_kernel(tc, r, B_bytes, B_scale, bias, seen, 
                 wide_t[c, g] = t
             for t in planes:
                 j = g * PACK + t
-                src = b_raw[c, g][:, t, :].bitcast(FP8)
+                src = b_raw[c, g][:, t, 0:w].bitcast(FP8)
                 dst = wide_t[c, g][:, t, :]
                 if t in V_PLANES[c]:
                     nc.vector.tensor_scalar(out=dst, in0=src, scalar1=sc[:, j:j + 1], scalar2=None, op0=MULT)
@@ -131,7 +158,12 @@ def tile_masked_item_recommender_d3_kernel(tc, r, B_bytes, B_scale, bias, seen, 
             nc.vector.quantize_mx(out=b_codes[c][:, g, :].bitcast(FP8X4), scales=b_scales[c][:, g, :],
                                   in_=grp_t[c, g][:].rearrange("p n t -> p (n t)"))
 
-        r_codes, r_scales, tp_t, rg_t = {}, {}, {}, {}
+        r_codes, r_scales, tp_t, rg_t = [], [], {}, {}
+        for h in range(2):
+            rct = keep.tile([P, GROUPS, HALF * P], U32, name="r_codes%d" % h, align_bytes=64)
+            rst = keep.tile([P, GROUPS, HALF * P], U8, name="r_scales%d" % h, align_bytes=64)
+            r_codes.append(rct)
+            r_scales.append(rst)
 
         def transposes(u):
             words = r_raw[u][:].bitcast(F32)
@@ -145,50 +177,65 @@ def tile_masked_item_recommender_d3_kernel(tc, r, B_bytes, B_scale, bias, seen, 
 
         def copy_r(u, h):
             if h == 0:
-                t = stage.tile([P, 2, 2 * P * PACK], BF16, name="r_grp", align_bytes=64)
+                t = stage.tile([P, GROUPS, P * PACK], BF16, name="r_grp", align_bytes=64)
                 rg_t[u] = t
-            dst = rg_t[u][:, h, :].bitcast(F32).rearrange("p (g n e) -> p g n e", g=2, e=2)
+            dst = rg_t[u][:, 2 * h:2 * h + 2, :].bitcast(F32).rearrange("p g (n e) -> p g n e", e=2)
             nc.scalar.copy(out=dst, in_=tp_t[u, h][:].rearrange("p g e n -> p g n e"))
 
         def quant_r(u):
-            ct = keep.tile([P, GROUPS, P], U32, name="r_codes%d" % u, align_bytes=64)
-            st = keep.tile([P, GROUPS, P], U8, name="r_scales%d" % u, align_bytes=64)
-            nc.vector.quantize_mx(out=ct[:].rearrange("p g n -> p (g n)").bitcast(FP8X4),
-                                  scales=st[:].rearrange("p g n -> p (g n)"),
-                                  in_=rg_t[u][:].rearrange("p h x -> p (h x)"))
-            r_codes[u], r_scales[u] = ct, st
+            h, q = divmod(u, HALF)
+            for g in range(GROUPS):
+                nc.vector.quantize_mx(out=r_codes[h][:, g, q * P:q * P + P].bitcast(FP8X4),
+                                      scales=r_scales[h][:, g, q * P:q * P + P], in_=rg_t[u][:, g, :])
 
         ub = const.tile([P, I], BF16, name="ub")
+        bias_col = const.tile([P, 8], F32, name="bias_col")
+        bias_ps = []
 
-        def spread_bias():
-            for q in range(4):
-                ps = psum.tile([P, 512], F32, name="ps")
-                nc.tensor.matmul(ps[:], lhsT=ones[:], rhs=bias_row[:, 512 * q:512 * q + 512], start=True, stop=True)
-                nc.vector.tensor_scalar(out=ub[:, 512 * q:512 * q + 512], in0=ps[:], scalar1=1.0 / MASK, scalar2=None, op0=MULT)
+        def spread_bias_mm():
+            for n, w in ((0, 256), (1280, 768)):
+                ps = psum.tile([P, 1024], BF16, name="ps")
+                for q in range(0, w, 512):
+                    ww = min(512, w - q)
+                    nc.tensor.matmul(ps[:, q:q + ww], lhsT=small[:], rhs=bias_row[:, n + q:n + q + ww], start=True, stop=True)
+                bias_ps.append((n, w, ps))
+            pc = psum.tile([P, 8], F32, name="ps")
+            for j in range(8):
+                nc.tensor.matmul(pc[:, j:j + 1], lhsT=bias_row[:, T0 + P * j:T0 + P * j + P], rhs=one[:, 0:1], start=True, stop=True)
+            bias_ps.append((0, 0, pc))
 
-        def mask(s, u):
-            n0, w = SEEN_CUTS[s]
-            nc.vector.tensor_tensor(out=w_t[s, u][:], in0=ub[:, n0:n0 + w], in1=w_t[s, u][:], op=SUB)
+        def spread_bias_copy():
+            for n, w, ps in bias_ps:
+                if w:
+                    nc.vector.tensor_copy(out=ub[:, n:n + w], in_=ps[:, 0:w])
+                else:
+                    nc.vector.tensor_copy(out=bias_col[:], in_=ps[:])
+
+        def mask(c, u):
+            n0, w = D_CUTS[c]
+            nc.vector.tensor_tensor(out=w_t[c, u][:], in0=ub[:, n0:n0 + w], in1=w_t[c, u][:], op=SUB)
+            if c == 3:
+                w_t[4, u] = w_t[3, u]
 
         z_t, a_t = {}, {}
 
         def mm(c, u):
             n0, w = CHUNKS[c]
+            h, q = divmod(u, HALF)
             z = psum.tile([P, 512], F32, name="ps")
             for g in range(GROUPS):
                 nc.tensor.matmul_mx(out=z[:, 0:w],
-                                    lhsT=r_codes[u][:, g, :].bitcast(FP8X4), lhsT_scale=r_scales[u][:, g, :],
+                                    lhsT=r_codes[h][:, g, q * P:q * P + P].bitcast(FP8X4), lhsT_scale=r_scales[h][:, g, q * P:q * P + P],
                                     rhs=b_codes[c][:, g, :].bitcast(FP8X4), rhs_scale=b_scales[c][:, g, :],
                                     start=(g == 0), stop=(g == GROUPS - 1))
             z_t[c, u] = z
 
         def add(c, u):
             n0, w = CHUNKS[c]
-            s = 0 if n0 < 768 else 1
-            off = n0 - SEEN_CUTS[s][0]
+            off = n0 - D_CUTS[c][0]
             a = outs.tile([P, 512], F32, name="arg")
             nc.vector.scalar_tensor_tensor(out=a[:, 0:w], in0=z_t[c, u][:, 0:w], scalar=1.0 / MASK,
-                                           in1=w_t[s, u][:, off:off + w], op0=MULT, op1=ADD)
+                                           in1=w_t[c, u][:, off:off + w], op0=MULT, op1=ADD)
             a_t[c, u] = a
 
         def expo(c, u):
@@ -197,58 +244,104 @@ def tile_masked_item_recommender_d3_kernel(tc, r, B_bytes, B_scale, bias, seen, 
             nc.scalar.activation(out=o[:, 0:w], in_=a_t[c, u][:, 0:w], func=ACT.Exp, scale=MASK)
             nc.sync.dma_start(out=out[u * P:(u + 1) * P, n0:n0 + w], in_=o[:, 0:w])
 
+        e_t, eT_t, o_t = {}, {}, {}
+
+        def mm_t(c, i):
+            h, j = divmod(i, 4)
+            z = psum.tile([P, 512], F32, name="ps")
+            for g in range(GROUPS):
+                nc.tensor.matmul_mx(out=z[:],
+                                    lhsT=b_codes[c][:, g, j * P:j * P + P].bitcast(FP8X4), lhsT_scale=b_scales[c][:, g, j * P:j * P + P],
+                                    rhs=r_codes[h][:, g, :].bitcast(FP8X4), rhs_scale=r_scales[h][:, g, :],
+                                    start=(g == 0), stop=(g == GROUPS - 1))
+            z_t[c, i] = z
+
+        def expo_t(c, i):
+            j = (CHUNKS[c][0] - T0) // P + i % 4
+            e = outs.tile([P, 512], F32, name="arg")
+            nc.scalar.activation(out=e[:], in_=z_t[c, i][:], func=ACT.Exp, bias=bias_col[:, j:j + 1], scale=1.0)
+            e_t[c, i] = e
+
+        def turn_t(c, i):
+            tp = psum.tile([P, HALF, P], F32, name="ps")
+            for q in range(HALF):
+                nc.tensor.transpose(tp[:, q, :], e_t[c, i][:, q * P:q * P + P], ident[:])
+            eT_t[c, i] = tp
+
+        def mask_t(c, i):
+            h, j = divmod(i, 4)
+            if j == 0:
+                ot = outs2.tile([P, HALF, 512], F32, name="o_t")
+                o_t[c, h] = ot
+            n = CHUNKS[c][0] - T0 + j * P
+            nc.vector.scalar_tensor_tensor(out=o_t[c, h][:, :, j * P:j * P + P], in0=seen_t[h][:, :, n:n + P], scalar=0.0,
+                                           in1=eT_t[c, i][:], op0=IS_EQUAL, op1=MULT)
+            if j == 3:
+                n0 = CHUNKS[c][0]
+                nc.sync.dma_start(out=out[h * HALF * P:(h + 1) * HALF * P, n0:n0 + 512].rearrange("(q p) n -> p q n", p=P), in_=o_t[c, h][:])
+
         for g in range(GROUPS):
             widen(0, g, range(4))
             if g >= 1:
                 interleave(0, g - 1)
             if g >= 2:
                 quant(0, g - 2)
-        transposes(0)
-        copy_r(0, 0)
-        copy_r(0, 1)
         interleave(0, 3)
         quant(0, 2)
-        spread_bias()
-        quant(0, 3)
-        quant_r(0)
-        mask(0, 0)
 
-        prev = None
-        for c in range(len(CHUNKS)):
-            for u in range(USERS):
+        tiles = [(c, u) for c in range(len(CHUNKS)) for u in range(USERS)]
+        n_t = len(tiles)
+
+        def tile_at(s, turned):
+            if 0 <= s < n_t and (tiles[s][0] in TURNED) == turned:
+                return [tiles[s]]
+            return []
+
+        for s in range(-LEAD, n_t + 5):
+            for rep in range(2 if s < 12 else 1):
                 if late:
                     late.pop(0)()
-                    if c == 0 and late:
-                        late.pop(0)()
-                nxt = c + 1 if c + 1 < len(CHUNKS) else None
-                g, half = u // 2, u % 2
-                if c == 0 and u + 1 < USERS:
-                    transposes(u + 1)
-                    copy_r(u + 1, 0)
-                    copy_r(u + 1, 1)
-                mm(c, u)
-                if nxt is not None:
-                    widen(nxt, g, (0, 1) if half == 0 else (2, 3))
-                if prev is not None:
-                    add(*prev)
-                if c == 0 and u + 1 < USERS:
-                    mask(0, u + 1)
-                    quant_r(u + 1)
-                if c == 1:
-                    mask(1, u)
-                if nxt is not None:
-                    if half == 0 and g >= 1:
-                        interleave(nxt, g - 1)
-                    if half == 1 and g >= 1:
-                        quant(nxt, g - 1)
-                if prev is not None:
-                    expo(*prev)
-                prev = (c, u)
-            if nxt is not None:
-                interleave(nxt, GROUPS - 1)
-                add(*prev)
-                quant(nxt, GROUPS - 1)
-                expo(*prev)
-                prev = None
-        add(*prev)
-        expo(*prev)
+            ru = s + TLEAD
+            if 0 <= ru < USERS:
+                transposes(ru)
+            if s % PAIR == 0:
+                for ss in range(s, s + PAIR):
+                    for t in tile_at(ss - LAG_TT, True):
+                        turn_t(*t)
+            for t in tile_at(s, False):
+                mm(*t)
+            for t in tile_at(s, True):
+                mm_t(*t)
+            if 0 <= ru < USERS:
+                copy_r(ru, 0)
+                copy_r(ru, 1)
+            for t in tile_at(s - LAG_TE, True):
+                expo_t(*t)
+            k, i = divmod(s + LEAD, USERS)
+            k += 1
+            if s == -LEAD:
+                quant(0, 3)
+                spread_bias_mm()
+                spread_bias_copy()
+            if k < len(CHUNKS):
+                g, half = divmod(i, 2)
+                widen(k, g, (0, 1) if half == 0 else (2, 3))
+            for t in tile_at(s - LAG_ADD, False):
+                add(*t)
+            for t in tile_at(s - LAG_TM, True):
+                mask_t(*t)
+            if 0 <= ru - 1 < USERS:
+                quant_r(ru - 1)
+                mask(0, ru - 1)
+            if 16 <= s < 24:
+                mask(3, s - 16)
+            pk, pi = divmod(s + LEAD - 2, USERS)
+            pk += 1
+            if 0 <= s + LEAD - 2 and pk < len(CHUNKS):
+                g, half = divmod(pi, 2)
+                if half == 0:
+                    interleave(pk, g)
+                else:
+                    quant(pk, g)
+            for t in tile_at(s - LAG_EXP, False):
+                expo(*t)

@@ -30,15 +30,15 @@ D_CUTS = {0: (0, 256), 3: (1280, 768), 4: (1280, 768)}
 T0, TW = 256, 1024
 MASK = 4096.0
 LEAD = 2
-LAG_ADD = 1
+LAG_ADD = 2
 LAG_EXP = 3
 LAG_TE = 1
 LAG_TT = 3
 LAG_TM = 3
 TLEAD = 2
 PAIR = 2
-B_BUFS = 13
-V_PLANES = [(0, 1), (), (0,), (), ()]
+V_PLANES = [(0, 1), (0,), (0,), (), ()]
+M3 = 12
 
 
 def tile_masked_item_recommender_d3_kernel(tc, r, B_bytes, B_scale, bias, seen, out):
@@ -46,8 +46,7 @@ def tile_masked_item_recommender_d3_kernel(tc, r, B_bytes, B_scale, bias, seen, 
     with ExitStack() as ctx:
         const = ctx.enter_context(tc.tile_pool(name="const", bufs=1))
         keep = ctx.enter_context(tc.tile_pool(name="keep", bufs=1))
-        raws = ctx.enter_context(tc.tile_pool(name="raws", bufs=6))
-        braws = ctx.enter_context(tc.tile_pool(name="braws", bufs=B_BUFS))
+        raws = ctx.enter_context(tc.tile_pool(name="raws", bufs=5))
         stage = ctx.enter_context(tc.tile_pool(name="stage", bufs=3))
         outs = ctx.enter_context(tc.tile_pool(name="outs", bufs=6))
         outs2 = ctx.enter_context(tc.tile_pool(name="outs2", bufs=2))
@@ -62,15 +61,19 @@ def tile_masked_item_recommender_d3_kernel(tc, r, B_bytes, B_scale, bias, seen, 
         bias_row = const.tile([P, I], BF16, name="bias_row")
         nc.vector.memset(bias_row[:].bitcast(I32), 0)
 
+        ctx.enter_context(tc.manual_schedule())
+
         sc = const.tile([P, GROUPS * PACK], F32, name="sc")
         bytes_view = B_bytes.rearrange("(g p t) n -> g p t n", p=P, t=PACK)
         b_raw = {}
 
-        def load_bytes(c, g):
-            n0, w = CHUNKS[c]
-            t8 = braws.tile([P, PACK, 512], U8, name="b_raw", align_bytes=64)
-            nc.sync.dma_start(out=t8[:, :, 0:w], in_=bytes_view[g][:, :, n0:n0 + w])
-            b_raw[c, g] = t8
+        def load_bytes(cs, g):
+            n0 = CHUNKS[cs[0]][0]
+            w = sum(CHUNKS[c][1] for c in cs)
+            t8 = keep.tile([P, PACK, w], U8, name="b_raw%d_%d" % (cs[0], g), align_bytes=64)
+            nc.sync.dma_start(out=t8[:], in_=bytes_view[g][:, :, n0:n0 + w])
+            for c in cs:
+                b_raw[c, g] = (t8, CHUNKS[c][0] - n0)
 
         r_raw = {}
 
@@ -99,33 +102,30 @@ def tile_masked_item_recommender_d3_kernel(tc, r, B_bytes, B_scale, bias, seen, 
         nc.scalar.dma_start(out=sc[:].rearrange("p (g t) -> p g t", t=PACK),
                             in_=B_scale.rearrange("(g p t) o -> p g (t o)", p=P, t=PACK))
         for g in range(GROUPS):
-            load_bytes(0, g)
+            load_bytes((0,), g)
         nc.sync.dma_start(out=bias_row[0:1, :], in_=bias.rearrange("(o n) -> o n", o=1))
         load_r(0)
-        load_bytes(1, 0)
+        load_bytes((1,), 0)
         load_r(1)
         load_seen(0, 0)
         load_r(2)
-        load_bytes(1, 1)
+        load_bytes((1,), 1)
         load_seen(0, 1)
         load_r(3)
-        load_bytes(1, 2)
+        load_bytes((1,), 2)
         load_seen(0, 2)
         load_r(4)
-        load_bytes(1, 3)
+        load_bytes((1,), 3)
         load_seen(0, 3)
 
         late = [lambda: load_r(5), lambda: load_seen(0, 4), lambda: load_r(6), lambda: load_seen(0, 5), lambda: load_r(7),
                 lambda: load_seen(0, 6), lambda: load_seen(0, 7)]
         for g in range(GROUPS):
-            late.append(lambda g=g: load_bytes(2, g))
+            late.append(lambda g=g: load_bytes((2, 3, 4), g))
             late.append(lambda q=g: load_seen_t(0, q))
         late += [lambda q=q: load_seen_t(1, q) for q in range(HALF)]
         for u in range(USERS):
-            if u % 2 == 0:
-                late.append(lambda g=u // 2: load_bytes(3, g))
             late.append(lambda u=u: load_seen(3, u))
-        late += [lambda g=g: load_bytes(4, g) for g in range(GROUPS)]
 
         b_codes, b_scales, wide_t, grp_t = {}, {}, {}, {}
         for c, (n0, w) in enumerate(CHUNKS):
@@ -140,7 +140,8 @@ def tile_masked_item_recommender_d3_kernel(tc, r, B_bytes, B_scale, bias, seen, 
                 wide_t[c, g] = t
             for t in planes:
                 j = g * PACK + t
-                src = b_raw[c, g][:, t, 0:w].bitcast(FP8)
+                t8, off = b_raw[c, g]
+                src = t8[:, t, off:off + w].bitcast(FP8)
                 dst = wide_t[c, g][:, t, :]
                 if t in V_PLANES[c]:
                     nc.vector.tensor_scalar(out=dst, in0=src, scalar1=sc[:, j:j + 1], scalar2=None, op0=MULT)
@@ -333,8 +334,8 @@ def tile_masked_item_recommender_d3_kernel(tc, r, B_bytes, B_scale, bias, seen, 
             if 0 <= ru - 1 < USERS:
                 quant_r(ru - 1)
                 mask(0, ru - 1)
-            if 16 <= s < 24:
-                mask(3, s - 16)
+            if M3 <= s < M3 + USERS:
+                mask(3, s - M3)
             pk, pi = divmod(s + LEAD - 2, USERS)
             pk += 1
             if 0 <= s + LEAD - 2 and pk < len(CHUNKS):

from contextlib import ExitStack

import concourse.mybir as mybir
from concourse.masks import make_identity

U, I = 1024, 2048
FLOPS = 2 * U * I * I

F32 = mybir.dt.float32
BF16 = mybir.dt.bfloat16
U32 = mybir.dt.uint32
I32 = mybir.dt.int32
U8 = mybir.dt.uint8
FP8 = mybir.dt.float8_e4m3fn
FP8X4 = mybir.dt.float8_e4m3fn_x4
MULT = mybir.AluOpType.mult
ADD = mybir.AluOpType.add
SUB = mybir.AluOpType.subtract
IS_EQUAL = mybir.AluOpType.is_equal
ACT = mybir.ActivationFunctionType

P = 128
PACK = 4
GROUPS = I // (P * PACK)
USERS = U // P
HALF = 4
CHUNKS = [(0, 256), (256, 512), (768, 512), (1280, 512), (1792, 256)]
TURNED = (1, 2)
D_CUTS = {0: (0, 256), 3: (1280, 768), 4: (1280, 768)}
T0, TW = 256, 1024
MASK = 4096.0
LEAD = 2
LAG_ADD = 2
LAG_EXP = 3
LAG_TE = 1
LAG_TT = 3
LAG_TM = 3
TLEAD = 2
PAIR = 2
V_PLANES = [(0, 1), (0,), (0,), (), ()]
M3 = 12


def tile_masked_item_recommender_d3_kernel(tc, r, B_bytes, B_scale, bias, seen, out):
    nc = tc.nc
    with ExitStack() as ctx:
        const = ctx.enter_context(tc.tile_pool(name="const", bufs=1))
        keep = ctx.enter_context(tc.tile_pool(name="keep", bufs=1))
        raws = ctx.enter_context(tc.tile_pool(name="raws", bufs=5))
        stage = ctx.enter_context(tc.tile_pool(name="stage", bufs=3))
        outs = ctx.enter_context(tc.tile_pool(name="outs", bufs=6))
        outs2 = ctx.enter_context(tc.tile_pool(name="outs2", bufs=2))
        psum = ctx.enter_context(tc.psum_pool(name="psum", bufs=8))

        ident = const.tile([P, P], F32, name="ident")
        make_identity(nc, ident[:])
        small = const.tile([P, P], BF16, name="small")
        nc.gpsimd.memset(small[:], 1.0 / MASK)
        one = const.tile([P, 2], BF16, name="one")
        nc.gpsimd.memset(one[:], 1.0)
        bias_row = const.tile([P, I], BF16, name="bias_row")
        nc.vector.memset(bias_row[:].bitcast(I32), 0)

        ctx.enter_context(tc.manual_schedule())

        sc = const.tile([P, GROUPS * PACK], F32, name="sc")
        bytes_view = B_bytes.rearrange("(g p t) n -> g p t n", p=P, t=PACK)
        b_raw = {}

        def load_bytes(cs, g):
            n0 = CHUNKS[cs[0]][0]
            w = sum(CHUNKS[c][1] for c in cs)
            t8 = keep.tile([P, PACK, w], U8, name="b_raw%d_%d" % (cs[0], g), align_bytes=64)
            nc.sync.dma_start(out=t8[:], in_=bytes_view[g][:, :, n0:n0 + w])
            for c in cs:
                b_raw[c, g] = (t8, CHUNKS[c][0] - n0)

        r_raw = {}

        def load_r(u):
            t = raws.tile([P, I], BF16, name="r_raw")
            nc.sync.dma_start(out=t[:], in_=r[u * P:(u + 1) * P, :])
            r_raw[u] = t

        w_t = {}

        def load_seen(c, u):
            n0, w = D_CUTS[c]
            t = keep.tile([P, w], BF16, name="seen%d_%d" % (c, u))
            nc.sync.dma_start(out=t[:], in_=seen[u * P:(u + 1) * P, n0:n0 + w])
            w_t[c, u] = t

        seen_t = []
        for h in range(2):
            sth = keep.tile([P, HALF, TW], BF16, name="seen_t%d" % h)
            seen_t.append(sth)

        def load_seen_t(h, q):
            u = HALF * h + q
            nc.sync.dma_start(out=seen_t[h][:, q, :], in_=seen[u * P:(u + 1) * P, T0:T0 + TW])

        nc.scalar.dma_start(out=sc[:].rearrange("p (g t) -> p g t", t=PACK),
                            in_=B_scale.rearrange("(g p t) o -> p g (t o)", p=P, t=PACK))
        for g in range(GROUPS):
            load_bytes((0,), g)
        nc.sync.dma_start(out=bias_row[0:1, :], in_=bias.rearrange("(o n) -> o n", o=1))
        load_r(0)
        load_bytes((1,), 0)
        load_r(1)
        load_seen(0, 0)
        load_r(2)
        load_bytes((1,), 1)
        load_seen(0, 1)
        load_r(3)
        load_bytes((1,), 2)
        load_seen(0, 2)
        load_r(4)
        load_bytes((1,), 3)
        load_seen(0, 3)

        late = [lambda: load_r(5), lambda: load_seen(0, 4), lambda: load_r(6), lambda: load_seen(0, 5), lambda: load_r(7),
                lambda: load_seen(0, 6), lambda: load_seen(0, 7)]
        for g in range(GROUPS):
            late.append(lambda g=g: load_bytes((2, 3, 4), g))
            late.append(lambda q=g: load_seen_t(0, q))
        late += [lambda q=q: load_seen_t(1, q) for q in range(HALF)]
        for u in range(USERS):
            late.append(lambda u=u: load_seen(3, u))

        b_codes, b_scales, wide_t, grp_t = {}, {}, {}, {}
        for c, (n0, w) in enumerate(CHUNKS):
            bct = keep.tile([P, GROUPS, w], U32, name="b_codes%d" % c, align_bytes=64)
            bst = keep.tile([P, GROUPS, w], U8, name="b_scales%d" % c, align_bytes=64)
            b_codes[c], b_scales[c] = bct, bst

        def widen(c, g, planes):
            n0, w = CHUNKS[c]
            if (c, g) not in wide_t:
                t = stage.tile([P, PACK, w], BF16, name="wide", align_bytes=64)
                wide_t[c, g] = t
            for t in planes:
                j = g * PACK + t
                t8, off = b_raw[c, g]
                src = t8[:, t, off:off + w].bitcast(FP8)
                dst = wide_t[c, g][:, t, :]
                if t in V_PLANES[c]:
                    nc.vector.tensor_scalar(out=dst, in0=src, scalar1=sc[:, j:j + 1], scalar2=None, op0=MULT)
                else:
                    nc.scalar.activation(out=dst, in_=src, func=ACT.Copy, scale=sc[:, j:j + 1])

        def interleave(c, g):
            n0, w = CHUNKS[c]
            t = stage.tile([P, w, PACK], BF16, name="grp", align_bytes=64)
            nc.vector.tensor_copy(out=t[:].rearrange("p (c i) t -> p c t i", i=4),
                                  in_=wide_t[c, g][:].rearrange("p t (c i) -> p c t i", i=4))
            grp_t[c, g] = t

        def quant(c, g):
            nc.vector.quantize_mx(out=b_codes[c][:, g, :].bitcast(FP8X4), scales=b_scales[c][:, g, :],
                                  in_=grp_t[c, g][:].rearrange("p n t -> p (n t)"))

        r_codes, r_scales, tp_t, rg_t = [], [], {}, {}
        for h in range(2):
            rct = keep.tile([P, GROUPS, HALF * P], U32, name="r_codes%d" % h, align_bytes=64)
            rst = keep.tile([P, GROUPS, HALF * P], U8, name="r_scales%d" % h, align_bytes=64)
            r_codes.append(rct)
            r_scales.append(rst)

        def transposes(u):
            words = r_raw[u][:].bitcast(F32)
            for h in range(2):
                tp = psum.tile([P, 2, 2, P], F32, name="ps")
                for gg in range(2):
                    for e in range(2):
                        k0 = 256 * (2 * h + gg)
                        nc.tensor.transpose(tp[:, gg, e, :], words[:, k0 + e:k0 + 256:2], ident[:])
                tp_t[u, h] = tp

        def copy_r(u, h):
            if h == 0:
                t = stage.tile([P, GROUPS, P * PACK], BF16, name="r_grp", align_bytes=64)
                rg_t[u] = t
            dst = rg_t[u][:, 2 * h:2 * h + 2, :].bitcast(F32).rearrange("p g (n e) -> p g n e", e=2)
            nc.scalar.copy(out=dst, in_=tp_t[u, h][:].rearrange("p g e n -> p g n e"))

        def quant_r(u):
            h, q = divmod(u, HALF)
            for g in range(GROUPS):
                nc.vector.quantize_mx(out=r_codes[h][:, g, q * P:q * P + P].bitcast(FP8X4),
                                      scales=r_scales[h][:, g, q * P:q * P + P], in_=rg_t[u][:, g, :])

        ub = const.tile([P, I], BF16, name="ub")
        bias_col = const.tile([P, 8], F32, name="bias_col")
        bias_ps = []

        def spread_bias_mm():
            for n, w in ((0, 256), (1280, 768)):
                ps = psum.tile([P, 1024], BF16, name="ps")
                for q in range(0, w, 512):
                    ww = min(512, w - q)
                    nc.tensor.matmul(ps[:, q:q + ww], lhsT=small[:], rhs=bias_row[:, n + q:n + q + ww], start=True, stop=True)
                bias_ps.append((n, w, ps))
            pc = psum.tile([P, 8], F32, name="ps")
            for j in range(8):
                nc.tensor.matmul(pc[:, j:j + 1], lhsT=bias_row[:, T0 + P * j:T0 + P * j + P], rhs=one[:, 0:1], start=True, stop=True)
            bias_ps.append((0, 0, pc))

        def spread_bias_copy():
            for n, w, ps in bias_ps:
                if w:
                    nc.vector.tensor_copy(out=ub[:, n:n + w], in_=ps[:, 0:w])
                else:
                    nc.vector.tensor_copy(out=bias_col[:], in_=ps[:])

        def mask(c, u):
            n0, w = D_CUTS[c]
            nc.vector.tensor_tensor(out=w_t[c, u][:], in0=ub[:, n0:n0 + w], in1=w_t[c, u][:], op=SUB)
            if c == 3:
                w_t[4, u] = w_t[3, u]

        z_t, a_t = {}, {}

        def mm(c, u):
            n0, w = CHUNKS[c]
            h, q = divmod(u, HALF)
            z = psum.tile([P, 512], F32, name="ps")
            for g in range(GROUPS):
                nc.tensor.matmul_mx(out=z[:, 0:w],
                                    lhsT=r_codes[h][:, g, q * P:q * P + P].bitcast(FP8X4), lhsT_scale=r_scales[h][:, g, q * P:q * P + P],
                                    rhs=b_codes[c][:, g, :].bitcast(FP8X4), rhs_scale=b_scales[c][:, g, :],
                                    start=(g == 0), stop=(g == GROUPS - 1))
            z_t[c, u] = z

        def add(c, u):
            n0, w = CHUNKS[c]
            off = n0 - D_CUTS[c][0]
            a = outs.tile([P, 512], F32, name="arg")
            nc.vector.scalar_tensor_tensor(out=a[:, 0:w], in0=z_t[c, u][:, 0:w], scalar=1.0 / MASK,
                                           in1=w_t[c, u][:, off:off + w], op0=MULT, op1=ADD)
            a_t[c, u] = a

        def expo(c, u):
            n0, w = CHUNKS[c]
            o = outs.tile([P, 512], F32, name="res")
            nc.scalar.activation(out=o[:, 0:w], in_=a_t[c, u][:, 0:w], func=ACT.Exp, scale=MASK)
            nc.sync.dma_start(out=out[u * P:(u + 1) * P, n0:n0 + w], in_=o[:, 0:w])

        e_t, eT_t, o_t = {}, {}, {}

        def mm_t(c, i):
            h, j = divmod(i, 4)
            z = psum.tile([P, 512], F32, name="ps")
            for g in range(GROUPS):
                nc.tensor.matmul_mx(out=z[:],
                                    lhsT=b_codes[c][:, g, j * P:j * P + P].bitcast(FP8X4), lhsT_scale=b_scales[c][:, g, j * P:j * P + P],
                                    rhs=r_codes[h][:, g, :].bitcast(FP8X4), rhs_scale=r_scales[h][:, g, :],
                                    start=(g == 0), stop=(g == GROUPS - 1))
            z_t[c, i] = z

        def expo_t(c, i):
            j = (CHUNKS[c][0] - T0) // P + i % 4
            e = outs.tile([P, 512], F32, name="arg")
            nc.scalar.activation(out=e[:], in_=z_t[c, i][:], func=ACT.Exp, bias=bias_col[:, j:j + 1], scale=1.0)
            e_t[c, i] = e

        def turn_t(c, i):
            tp = psum.tile([P, HALF, P], F32, name="ps")
            for q in range(HALF):
                nc.tensor.transpose(tp[:, q, :], e_t[c, i][:, q * P:q * P + P], ident[:])
            eT_t[c, i] = tp

        def mask_t(c, i):
            h, j = divmod(i, 4)
            if j == 0:
                ot = outs2.tile([P, HALF, 512], F32, name="o_t")
                o_t[c, h] = ot
            n = CHUNKS[c][0] - T0 + j * P
            nc.vector.scalar_tensor_tensor(out=o_t[c, h][:, :, j * P:j * P + P], in0=seen_t[h][:, :, n:n + P], scalar=0.0,
                                           in1=eT_t[c, i][:], op0=IS_EQUAL, op1=MULT)
            if j == 3:
                n0 = CHUNKS[c][0]
                nc.sync.dma_start(out=out[h * HALF * P:(h + 1) * HALF * P, n0:n0 + 512].rearrange("(q p) n -> p q n", p=P), in_=o_t[c, h][:])

        for g in range(GROUPS):
            widen(0, g, range(4))
            if g >= 1:
                interleave(0, g - 1)
            if g >= 2:
                quant(0, g - 2)
        interleave(0, 3)
        quant(0, 2)

        tiles = [(c, u) for c in range(len(CHUNKS)) for u in range(USERS)]
        n_t = len(tiles)

        def tile_at(s, turned):
            if 0 <= s < n_t and (tiles[s][0] in TURNED) == turned:
                return [tiles[s]]
            return []

        for s in range(-LEAD, n_t + 5):
            for rep in range(2 if s < 12 else 1):
                if late:
                    late.pop(0)()
            ru = s + TLEAD
            if 0 <= ru < USERS:
                transposes(ru)
            if s % PAIR == 0:
                for ss in range(s, s + PAIR):
                    for t in tile_at(ss - LAG_TT, True):
                        turn_t(*t)
            for t in tile_at(s, False):
                mm(*t)
            for t in tile_at(s, True):
                mm_t(*t)
            if 0 <= ru < USERS:
                copy_r(ru, 0)
                copy_r(ru, 1)
            for t in tile_at(s - LAG_TE, True):
                expo_t(*t)
            k, i = divmod(s + LEAD, USERS)
            k += 1
            if s == -LEAD:
                quant(0, 3)
                spread_bias_mm()
                spread_bias_copy()
            if k < len(CHUNKS):
                g, half = divmod(i, 2)
                widen(k, g, (0, 1) if half == 0 else (2, 3))
            for t in tile_at(s - LAG_ADD, False):
                add(*t)
            for t in tile_at(s - LAG_TM, True):
                mask_t(*t)
            if 0 <= ru - 1 < USERS:
                quant_r(ru - 1)
                mask(0, ru - 1)
            if M3 <= s < M3 + USERS:
                mask(3, s - M3)
            pk, pi = divmod(s + LEAD - 2, USERS)
            pk += 1
            if 0 <= s + LEAD - 2 and pk < len(CHUNKS):
                g, half = divmod(pi, 2)
                if half == 0:
                    interleave(pk, g)
                else:
                    quant(pk, g)
            for t in tile_at(s - LAG_EXP, False):
                expo(*t)
